import numpy as np
import ml_dtypes


def mxq(x, axis, fmt="e4m3"):
    dtype, down = {"e4m3": (ml_dtypes.float8_e4m3fn, 7), "e5m2": (ml_dtypes.float8_e5m2, 14)}[fmt]
    v = np.moveaxis(np.asarray(x, np.float32).astype(ml_dtypes.bfloat16).astype(np.float64), axis, -1)
    blocks = v.reshape(v.shape[:-1] + (-1, 32))
    amax = np.abs(blocks).max(-1, keepdims=True)
    byte = np.maximum(np.where(amax > 0, np.frexp(amax)[1] - 1 + 127, 0) - down, 1)
    scale = np.exp2(byte - 127.0)
    codes = (blocks / scale).astype(np.float32).astype(dtype).astype(np.float64)
    return np.moveaxis((codes * scale).reshape(v.shape), -1, axis)


WIDE = False


def mx_kscale(k):
    if not WIDE:
        return np.ones(k)
    levels = np.array([10, -10, 5, -5, 0])
    if k % 512:
        return np.exp2(np.random.permutation(np.resize(levels, k // 32))).repeat(32)
    a = np.empty((k // 512, 16))
    for p in range(k // 512):
        a[p, :8] = np.random.permutation(np.resize(levels, 8))
        for g in range(8):
            far = levels[np.abs(levels - a[p, g]) >= 10]
            a[p, g + 8] = far[np.random.randint(len(far))]
    return np.exp2(a.ravel()).repeat(32)


def f64(x):
    return np.asarray(x).astype(np.float64)


def striped(idx):
    return np.tile(idx.reshape(-1, 16).T, (8, 1)).astype(np.uint16)


def unstriped(offs):
    return offs[:16].T.reshape(-1).astype(np.int64)


def striped8(idx):
    return np.concatenate([x.reshape(-1, 16).T for x in idx]).astype(np.uint16)


def runs(offs, k):
    lists = np.stack([offs[16 * r : 16 * r + 16].T.reshape(-1) for r in range(8)]).astype(np.int64)
    return lists[np.arange(k) % 512 // 64]


def pack_weight(w):
    k, n = w.shape
    w = f64(np.asarray(w, np.float32).astype(ml_dtypes.bfloat16)).reshape(k // 32, 32, n)
    amax = np.abs(w).max(1)
    byte = np.clip(np.where(amax > 0, np.frexp(amax)[1] - 1 + 127 - 7, 1), 1, 254)
    scaled = (w * np.exp2(127.0 - byte)[:, None, :]).reshape(k, n).astype(np.float32)
    words = np.ascontiguousarray(scaled.reshape(k // 512, 128, 4, n).transpose(0, 1, 3, 2)).astype(ml_dtypes.float8_e4m3fn).view(np.uint8)
    return words, np.ascontiguousarray(byte.astype(np.uint8).reshape(k // 512, 16, n))


def unpack_weight(words, scales):
    g, p, n, _ = words.shape
    vals = np.ascontiguousarray(words).view(ml_dtypes.float8_e4m3fn).astype(np.float64) * np.repeat(np.exp2(scales.astype(np.float64) - 127.0), 8, axis=1)[..., None]
    return vals.transpose(0, 1, 3, 2).reshape(g * 512, n)


E2M1 = np.array([0.0, 0.5, 1.0, 1.5, 2.0, 3.0, 4.0, 6.0, -0.0, -0.5, -1.0, -1.5, -2.0, -3.0, -4.0, -6.0])


def pack_fp4(w):
    k, n = w.shape
    w = f64(np.asarray(w, np.float32).astype(ml_dtypes.bfloat16)).reshape(k // 32, 32, n)
    amax = np.abs(w).max(1)
    mant, ex = np.frexp(amax / 6.0)
    byte = np.clip(np.where(amax > 0, np.where(mant > 0.5, ex, ex - 1) + 127, 1), 1, 254)
    scaled = (w * np.exp2(127.0 - byte)[:, None, :]).reshape(k, n).astype(np.float32)
    c = np.ascontiguousarray(scaled.reshape(k // 512, 128, 4, n).transpose(0, 1, 3, 2)).astype(ml_dtypes.float4_e2m1fn).view(np.uint8) & 0xF
    words = (c[..., 0::2] | (c[..., 1::2] << 4)).reshape(k // 512, 128, 2 * n)
    return np.ascontiguousarray(words), np.ascontiguousarray(byte.astype(np.uint8).reshape(k // 512, 16, n))


def unpack_fp4(words, scales):
    g, _, n = scales.shape
    words = np.ascontiguousarray(words).reshape(g, 128, n, 2)
    nib = np.empty((g, 128, n, 4), np.uint8)
    nib[..., 0::2] = words & 0xF
    nib[..., 1::2] = words >> 4
    vals = E2M1[nib] * np.repeat(np.exp2(scales.astype(np.float64) - 127.0), 8, axis=1)[..., None]
    return vals.transpose(0, 1, 3, 2).reshape(g * 512, n)


def planes(y):
    n, m = y.shape
    v = y.astype(np.float32).astype(ml_dtypes.bfloat16).astype(np.float64).reshape(n // 32, 32, m)
    top = np.abs(v).max(1)
    byte = np.clip(np.where(top > 0, np.frexp(top)[1] - 1 + 127 - 7, 1), 1, 254)
    codes = (v * np.exp2(127.0 - byte)[:, None, :]).reshape(n, m).astype(np.float32).astype(ml_dtypes.float8_e4m3fn).view(np.uint8)
    words = codes.reshape(n // 512, 128, 4, m).transpose(0, 1, 3, 2)
    return np.ascontiguousarray(words), np.ascontiguousarray(byte.astype(np.uint8).reshape(n // 512, 16, m))


K, T, S, H, G = 512, 1024, 512, 512, 2048


def setup_inputs():
    n = np.random.standard_normal
    s = mx_kscale(K)[:, None]
    packed_xT = pack_weight(n((K, T)) * s)
    packed_w1 = pack_fp4(n((K, H)) / np.sqrt(K) / s)
    packed_w2 = pack_fp4(n((K, H)) / np.sqrt(K) / s)
    packed_dT = pack_weight(n((K, G)) / s)
    return {
        "x_words": packed_xT[0],
        "x_scales": packed_xT[1],
        "w1_words": packed_w1[0],
        "w1_scales": packed_w1[1],
        "w2_words": packed_w2[0],
        "w2_scales": packed_w2[1],
        "gs": (np.random.uniform(0.5, 1.5, (K, 1)) * s).astype(np.float32),
        "d_words": packed_dT[0],
        "d_scales": packed_dT[1],
        "offs": striped(np.random.permutation(T)[:S]),
        "two": striped(np.random.permutation(T)[:S]),
        "n1": striped8(np.stack([np.random.permutation(S) for _ in range(8)])),
        "n2": striped8(np.stack([np.random.permutation(S) for _ in range(8)])),
        "n3": striped8(np.stack([np.random.permutation(S) for _ in range(8)])),
        "k1": striped8(np.random.randint(0, G, (8, H))),
        "n4": striped8(np.stack([np.random.permutation(S) for _ in range(8)])),
        "n5": striped8(np.stack([np.random.permutation(S) for _ in range(8)])),
    }


def reference(x_words, x_scales, w1_words, w1_scales, w2_words, w2_scales, gs, d_words, d_scales, offs, two, n1, n2, n3, k1, n4, n5):
    d_k1 = unpack_weight(d_words, d_scales)[np.arange(K)[:, None], runs(k1, K)]
    xq = unpack_weight(x_words, x_scales)[:, unstriped(offs)]
    y = unpack_fp4(w1_words, w1_scales).T @ xq
    x_two = unpack_weight(x_words, x_scales)[:, unstriped(two)]
    d = unpack_fp4(w2_words, w2_scales).T @ x_two
    z = f64(gs) * (np.maximum(np.minimum(y - (0.5 * (y[np.arange(H)[:, None], runs(n1, H)])), d[np.arange(H)[:, None], runs(n2, H)]), d[np.arange(H)[:, None], runs(n3, H)]))
    h = 0.0625 * ((d_k1.T @ mxq(z, 0, "e4m3")))
    st = np.maximum(h, h[np.arange(H)[:, None], runs(n4, H)])
    out_0 = st[np.arange(H)[:, None], runs(n5, H)] - (0.5 * h)
    return (out_0,) + planes(out_0)

@@ -1,0 +1,283 @@
+from contextlib import ExitStack
+
+import concourse.mybir as mybir
+from concourse.masks import make_identity
+
+F32 = mybir.dt.float32
+BF16 = mybir.dt.bfloat16
+I32 = mybir.dt.int32
+U32 = mybir.dt.uint32
+U16 = mybir.dt.uint16
+U8 = mybir.dt.uint8
+FP8X4 = mybir.dt.float8_e4m3fn_x4
+FP4X4 = mybir.dt.float4_e2m1fn_x4
+ALU = mybir.AluOpType
+COPY = mybir.ActivationFunctionType.Copy
+
+P = 128
+PACK = 4
+K, T, S, H, G = 512, 1024, 512, 512, 2048
+FLOPS = 3 * 2 * K * H * S
+WIDE = 2 * S
+Z_CHUNKS = ((0, 256), (256, 512))
+OUT_CHUNKS = ((0, 256), (256, 384), (384, 512))
+
+
+def load_scale_rows(queue, plane, rows):
+    for q in range(4):
+        four = rows[4 * q : 4 * q + 4, :].bitcast(I32)
+        queue.dma_start(out=plane[32 * q : 32 * q + 32, :].bitcast(I32), in_=four.unsqueeze(0).to_broadcast([8, 4, four.shape[1]]))
+
+
+def load_live_rows(queue, plane, rows):
+    for q in range(4):
+        queue.dma_start(out=plane[32 * q : 32 * q + 4, :].bitcast(I32), in_=rows[4 * q : 4 * q + 4, :].bitcast(I32))
+
+
+def tile_picked_twqclampbhopb_none_po_kernel(
+    tc, x_words, x_scales, w1_words, w1_scales, w2_words, w2_scales, gs, d_words, d_scales,
+    offs, two, n1, n2, n3, k1, n4, n5, out_0, out_1, out_2,
+):
+    nc = tc.nc
+    with ExitStack() as ctx:
+        lists = ctx.enter_context(tc.tile_pool(name="lists", bufs=1))
+        keep = ctx.enter_context(tc.tile_pool(name="keep", bufs=1))
+        work = ctx.enter_context(tc.tile_pool(name="work", bufs=2))
+        psum = ctx.enter_context(tc.psum_pool(name="psum", bufs=8))
+
+        def load_list(name, source):
+            tile = lists.tile([P, S // 16], U16, name=name)
+            nc.sync.dma_start(tile[:], source)
+            return tile
+
+        def zeroed_bytes(name, width, engine):
+            tile = keep.tile([P, width], U8, name=name, align_bytes=64)
+            engine.memset(tile[:].bitcast(I32), 0)
+            return tile
+
+        identity = keep.tile([P, P], F32, name="identity")
+        make_identity(nc, identity[:])
+        x_byte_table = keep.tile([P, T], U8, name="x_byte_table", align_bytes=64)
+        w2_plane = keep.tile([P, H], U8, name="w2_plane", align_bytes=64)
+        w1_plane = keep.tile([P, H], U8, name="w1_plane", align_bytes=64)
+        d_byte_table = zeroed_bytes("d_byte_table", G, nc.vector)
+        code_plane = zeroed_bytes("code_plane", H, nc.vector)
+
+        two_list = load_list("two_list", two)
+        x_word_table = keep.tile([P, T], U32, name="x_word_table", align_bytes=64)
+        load_scale_rows(nc.sync, x_byte_table, x_scales[0])
+        nc.sync.dma_start(out=x_word_table[:].bitcast(I32), in_=x_words[0].rearrange("p c r -> p (c r)").bitcast(I32))
+        w2_raw_words = keep.tile([P, 2 * H], U8, name="w2_raw_words", align_bytes=64)
+        nc.sync.dma_start(out=w2_raw_words[:].bitcast(I32), in_=w2_words[0].bitcast(I32))
+        offs_list = load_list("offs_list", offs)
+        load_live_rows(nc.sync, w2_plane, w2_scales[0])
+        w1_raw_words = keep.tile([P, 2 * H], U8, name="w1_raw_words", align_bytes=64)
+        nc.sync.dma_start(out=w1_raw_words[:].bitcast(I32), in_=w1_words[0].bitcast(I32))
+        load_live_rows(nc.sync, w1_plane, w1_scales[0])
+        k1_list = load_list("k1_list", k1)
+        d_rows = d_scales[0].rearrange("(r e) c -> e r c", e=2)
+        for e in range(2):
+            nc.sync.dma_start(out=d_byte_table[e:P:16, :].bitcast(I32), in_=d_rows[e].bitcast(I32))
+        n2_list = load_list("n2_list", n2)
+        n3_list = load_list("n3_list", n3)
+        n1_list = load_list("n1_list", n1)
+        gain = keep.tile([P, PACK], F32, name="gain")
+        nc.sync.dma_start(out=gain[:], in_=gs.rearrange("(p t) o -> p (t o)", t=PACK))
+        d_word_table = keep.tile([P, G], U32, name="d_word_table", align_bytes=64)
+        nc.sync.dma_start(out=d_word_table[:].bitcast(I32), in_=d_words[0].rearrange("p c r -> p (c r)").bitcast(I32))
+        n4_list = load_list("n4_list", n4)
+        n5_list = load_list("n5_list", n5)
+
+        def pick(name, table, offsets, dtype):
+            tile = keep.tile([P, S], dtype, name=name, align_bytes=64)
+            nc.vector.tensor_copy(tile[:], table[:].indirect(offsets[:]))
+            return tile
+
+        def deal(name, source, per_column, dtype):
+            tile = keep.tile([P, H * per_column], dtype, name=name, align_bytes=64)
+            nc.vector.tensor_copy(
+                tile[:].rearrange("p (t m b) -> p t m b", t=PACK, b=per_column),
+                source[:].rearrange("p (m t b) -> p t m b", t=PACK, b=per_column),
+            )
+            return tile
+
+        def turned_product(name, words, plane, token_list):
+            token_bytes = pick(name + "_token_bytes", x_byte_table, token_list, U8)
+            token_words = pick(name + "_token_words", x_word_table, token_list, U32)
+            turned = []
+            for u in range(S // P):
+                bank = psum.tile([P, H], F32, name="bank")
+                nc.tensor.matmul_mx(
+                    out=bank[:],
+                    lhsT=token_words[:, P * u : P * (u + 1)].bitcast(FP8X4),
+                    lhsT_scale=token_bytes[:, P * u : P * (u + 1)],
+                    rhs=words[:].bitcast(FP4X4),
+                    rhs_scale=plane[:],
+                    start=True,
+                    stop=True,
+                )
+                dealt = keep.tile([P, PACK, P], F32, name="%s_turned%d" % (name, u))
+                nc.scalar.copy(dealt[:], bank[:].rearrange("p (m t) -> p t m", t=PACK))
+                turned.append(dealt)
+            return turned
+
+        def turn_back(turned, t):
+            bank = psum.tile([P, S], F32, name="bank")
+            for u in range(S // P):
+                nc.tensor.transpose(bank[:, P * u : P * (u + 1)], turned[u][:, t, :], identity[:])
+            return bank
+
+        d_win, y_win, y_plain = [], [], []
+
+        def d_rows_out(t):
+            bank = turn_back(d_turned, t)
+            win = keep.tile([P, WIDE], F32, name="d_win%d" % t)
+            nc.scalar.copy(win[:, :S], bank[:])
+            d_win.append(win)
+
+        def y_rows_out(t):
+            bank = turn_back(y_turned, t)
+            win = keep.tile([P, WIDE], F32, name="y_win%d" % t)
+            plain = keep.tile([P, S], F32, name="y_plain%d" % t)
+            nc.scalar.activation(win[:, :S], bank[:], COPY, scale=-0.5)
+            nc.scalar.copy(plain[:], bank[:])
+            y_win.append(win)
+            y_plain.append(plain)
+
+        d_turned = turned_product("w2", w2_raw_words, w2_plane, two_list)
+        d_rows_out(0)
+        d_rows_out(1)
+        y_turned = turned_product("w1", w1_raw_words, w1_plane, offs_list)
+        y_rows_out(0)
+        d_rows_out(2)
+        y_rows_out(1)
+        d_rows_out(3)
+        y_rows_out(2)
+        y_rows_out(3)
+
+        code_bytes = pick("code_bytes", d_byte_table, k1_list, U8)
+        code_dealt_bytes = deal("code_dealt_bytes", code_bytes, 1, U8)
+        for row, part in enumerate((0, 1, 16, 17)):
+            nc.sync.dma_start(out=code_plane[row:P:32, :].bitcast(I32), in_=code_dealt_bytes[part:P:32, :].bitcast(I32))
+
+        z_bf = keep.tile([P, S, PACK], BF16, name="z_bf", align_bytes=64)
+        units = [(t, 0, S) for t in range(PACK - 1)] + [(PACK - 1, lo, hi) for lo, hi in Z_CHUNKS]
+        got = {}
+
+        def look_up_d(i):
+            t, lo, hi = units[i]
+            last = i == len(units) - 1
+            at_n2 = keep.tile([P, hi - lo], F32, name="at_n2_%d" % i, tag="held" if last else "at_n2_%d" % i, align_bytes=64)
+            at_n3 = keep.tile([P, hi - lo], F32, name="at_n3_%d" % i)
+            nc.vector.tensor_copy(at_n2[:], d_win[t][:].indirect(n2_list[:, lo // 16 : hi // 16]))
+            nc.vector.tensor_copy(at_n3[:], d_win[t][:].indirect(n3_list[:, lo // 16 : hi // 16]))
+            got["n2", i] = at_n2
+            got["n3", i] = at_n3
+
+        def look_up_y(i):
+            t, lo, hi = units[i]
+            lessened = keep.tile([P, hi - lo], F32, name="lessened%d" % i)
+            nc.vector.tensor_tensor(
+                lessened[:], y_win[t][:].indirect(n1_list[:, lo // 16 : hi // 16]), y_plain[t][:, lo:hi], ALU.add
+            )
+            got["n1", i] = lessened
+
+        def smaller(i):
+            t, lo, hi = units[i]
+            low = keep.tile([P, hi - lo], F32, name="low%d" % i)
+            nc.vector.tensor_tensor(low[:], got["n1", i][:], got["n2", i][:], ALU.min)
+            got["low", i] = low
+
+        def larger(i):
+            t, lo, hi = units[i]
+            clamped = keep.tile([P, hi - lo], F32, name="clamped%d" % i)
+            nc.vector.tensor_tensor(clamped[:], got["low", i][:], got["n3", i][:], ALU.max)
+            nc.scalar.activation(z_bf[:, lo:hi, t], clamped[:], COPY, scale=gain[:, t : t + 1])
+
+        z_words = keep.tile([P, S], U32, name="z_words", align_bytes=64)
+        z_plane = keep.tile([P, S], U8, name="z_plane", align_bytes=64)
+
+        def quantise_z(lo, hi):
+            nc.vector.quantize_mx(
+                out=z_words[:, lo:hi].bitcast(FP8X4),
+                scales=z_plane[:, lo:hi],
+                in_=z_bf[:, lo:hi, :].rearrange("p j t -> p (j t)"),
+            )
+
+        look_up_d(0)
+        for i in range(len(units)):
+            if i + 1 < len(units):
+                look_up_d(i + 1)
+            look_up_y(i)
+            if i > 0:
+                larger(i - 1)
+            smaller(i)
+        larger(len(units) - 1)
+        code_words = keep.tile([P, S], U32, name="code_words", tag="held", align_bytes=64)
+        nc.vector.tensor_copy(code_words[:], d_word_table[:].indirect(k1_list[:]))
+        quantise_z(*Z_CHUNKS[0])
+        code_dealt = deal("code_dealt", code_words, 1, U32)
+        quantise_z(*Z_CHUNKS[1])
+
+        h_win, h_half = [], []
+        for t in range(PACK):
+            bank = psum.tile([P, S], F32, name="bank")
+            win = keep.tile([P, WIDE], F32, name="h_win%d" % t)
+            half = keep.tile([P, S], F32, name="h_half%d" % t)
+            for lo, hi in Z_CHUNKS:
+                nc.tensor.matmul_mx(
+                    out=bank[:, lo:hi],
+                    lhsT=code_dealt[:, P * t : P * (t + 1)].bitcast(FP8X4),
+                    lhsT_scale=code_plane[:, P * t : P * (t + 1)],
+                    rhs=z_words[:, lo:hi].bitcast(FP8X4),
+                    rhs_scale=z_plane[:, lo:hi],
+                    start=True,
+                    stop=True,
+                )
+            nc.scalar.activation(win[:, :S], bank[:], COPY, scale=0.0625)
+            h_win.append(win)
+            h_half.append((half, bank))
+        for half, bank in h_half:
+            nc.scalar.activation(half[:], bank[:], COPY, scale=0.03125)
+
+        st_win = []
+        at_n4 = []
+        for t in range(PACK + 1):
+            if t < PACK:
+                got = work.tile([P, S], F32, name="at_n4")
+                nc.vector.tensor_copy(got[:], h_win[t][:].indirect(n4_list[:]))
+                at_n4.append(got)
+            if t > 0:
+                win = keep.tile([P, S], F32, name="st_win%d" % (t - 1))
+                nc.vector.tensor_tensor(win[:], at_n4[t - 1][:], h_win[t - 1][:, :S], ALU.max)
+                st_win.append(win)
+
+        out_rows = out_0.rearrange("(p t) j -> p t j", t=PACK)
+        out_words = out_1[0].rearrange("p c r -> p (c r)").bitcast(I32)
+        o_plane = keep.tile([P, S], U8, name="o_plane", align_bytes=64)
+        pending = None
+        for c, (lo, hi) in enumerate(OUT_CHUNKS):
+            n = hi - lo
+            result = keep.tile([P, PACK, n], F32, name="result%d" % c)
+            rounded = keep.tile([P, n, PACK], BF16, name="rounded%d" % c, align_bytes=64)
+            o_words = keep.tile([P, n], U32, name="o_words%d" % c, align_bytes=64)
+            for t in range(PACK):
+                nc.vector.tensor_tensor(
+                    result[:, t, :], st_win[t][:].indirect(n5_list[:, lo // 16 : hi // 16]), h_half[t][0][:, lo:hi], ALU.subtract
+                )
+                nc.scalar.copy(rounded[:, :, t], result[:, t, :])
+                if t == 2 and pending is not None:
+                    pending()
+            nc.sync.dma_start(out=out_rows[:, :, lo:hi], in_=result[:])
+
+            def quantise(lo=lo, hi=hi, rounded=rounded, o_words=o_words):
+                nc.vector.quantize_mx(
+                    out=o_words[:].bitcast(FP8X4), scales=o_plane[:, lo:hi], in_=rounded[:].rearrange("p j t -> p (j t)")
+                )
+                nc.sync.dma_start(out=out_words[:, lo:hi], in_=o_words[:].bitcast(I32))
+
+            pending = quantise
+        pending()
+        for q in range(4):
+            queue = nc.scalar if q % 2 else nc.sync
+            queue.dma_start(out=out_2[0][4 * q : 4 * q + 4, :].bitcast(I32), in_=o_plane[32 * q : 32 * q + 4, :].bitcast(I32))

@@ -15,23 +15,29 @@ ALU = mybir.AluOpType
 COPY = mybir.ActivationFunctionType.Copy
 
 P = 128
-PACK = 4
+SLOTS = 4
+LAST = SLOTS - 1
+PER_COLUMN = 16
 K, T, S, H, G = 512, 1024, 512, 512, 2048
 FLOPS = 3 * 2 * K * H * S
+
 WIDE = 2 * S
-Z_CHUNKS = ((0, 256), (256, 512))
-OUT_CHUNKS = ((0, 256), (256, 384), (384, 512))
+HALF = S // 2
+WHOLE = ((0, S),)
+HALVES = ((0, HALF), (HALF, S))
+CHUNKS = ((0, HALF), (HALF, HALF + P), (HALF + P, S))
 
 
-def load_scale_rows(queue, plane, rows):
-    for q in range(4):
-        four = rows[4 * q : 4 * q + 4, :].bitcast(I32)
-        queue.dma_start(out=plane[32 * q : 32 * q + 32, :].bitcast(I32), in_=four.unsqueeze(0).to_broadcast([8, 4, four.shape[1]]))
+def plane_rows(plane, rows):
+    return [(plane[32 * q : 32 * q + 4, :].bitcast(I32), rows[4 * q : 4 * q + 4, :].bitcast(I32)) for q in range(4)]
 
 
-def load_live_rows(queue, plane, rows):
-    for q in range(4):
-        queue.dma_start(out=plane[32 * q : 32 * q + 4, :].bitcast(I32), in_=rows[4 * q : 4 * q + 4, :].bitcast(I32))
+def word_rows(words):
+    return words.rearrange("p c r -> p (c r)").bitcast(I32)
+
+
+def places(offsets, lo, hi):
+    return offsets[:, lo // PER_COLUMN : hi // PER_COLUMN]
 
 
 def tile_picked_twqclampbhopb_none_po_kernel(
@@ -42,242 +48,238 @@ def tile_picked_twqclampbhopb_none_po_kernel(
     with ExitStack() as ctx:
         lists = ctx.enter_context(tc.tile_pool(name="lists", bufs=1))
         keep = ctx.enter_context(tc.tile_pool(name="keep", bufs=1))
-        work = ctx.enter_context(tc.tile_pool(name="work", bufs=2))
-        psum = ctx.enter_context(tc.psum_pool(name="psum", bufs=8))
+        psum = ctx.enter_context(tc.psum_pool(name="psum", bufs=1))
 
-        def load_list(name, source):
-            tile = lists.tile([P, S // 16], U16, name=name)
-            nc.sync.dma_start(tile[:], source)
-            return tile
+        def sbuf(name, shape, dtype, tag=None):
+            return keep.tile(shape, dtype, name=name, tag=tag or name, align_bytes=64)
+
+        def bank(number, width):
+            return psum.tile([P, width], F32, name="bank%d" % number)
 
         def zeroed_bytes(name, width, engine):
-            tile = keep.tile([P, width], U8, name=name, align_bytes=64)
+            tile = sbuf(name, [P, width], U8)
             engine.memset(tile[:].bitcast(I32), 0)
             return tile
 
-        identity = keep.tile([P, P], F32, name="identity")
+        def load(name, shape, dtype, source):
+            tile = sbuf(name, shape, dtype)
+            nc.sync.dma_start(out=tile[:].bitcast(I32), in_=source)
+            return tile
+
+        def load_list(name, source):
+            tile = lists.tile([P, S // PER_COLUMN], U16, name=name)
+            nc.sync.dma_start(tile[:], source)
+            return tile
+
+        def load_plane(plane, rows):
+            for partitions, source in plane_rows(plane, rows):
+                nc.sync.dma_start(out=partitions, in_=source)
+
+        def quantise(words, plane, rounded):
+            nc.vector.quantize_mx(out=words.bitcast(FP8X4), scales=plane, in_=rounded[:].rearrange("p j t -> p (j t)"))
+
+        x_byte_table = zeroed_bytes("x_byte_table", T, nc.gpsimd)
+        identity = sbuf("identity", [P, P], F32)
         make_identity(nc, identity[:])
-        x_byte_table = keep.tile([P, T], U8, name="x_byte_table", align_bytes=64)
-        w2_plane = keep.tile([P, H], U8, name="w2_plane", align_bytes=64)
-        w1_plane = keep.tile([P, H], U8, name="w1_plane", align_bytes=64)
         d_byte_table = zeroed_bytes("d_byte_table", G, nc.vector)
         code_plane = zeroed_bytes("code_plane", H, nc.vector)
 
+        w2_codes = load("w2_codes", [P, 2 * H], U8, w2_words[0].bitcast(I32))
         two_list = load_list("two_list", two)
-        x_word_table = keep.tile([P, T], U32, name="x_word_table", align_bytes=64)
-        load_scale_rows(nc.sync, x_byte_table, x_scales[0])
-        nc.sync.dma_start(out=x_word_table[:].bitcast(I32), in_=x_words[0].rearrange("p c r -> p (c r)").bitcast(I32))
-        w2_raw_words = keep.tile([P, 2 * H], U8, name="w2_raw_words", align_bytes=64)
-        nc.sync.dma_start(out=w2_raw_words[:].bitcast(I32), in_=w2_words[0].bitcast(I32))
+        load_plane(x_byte_table, x_scales[0])
+        x_word_table = load("x_word_table", [P, T], U32, word_rows(x_words[0]))
         offs_list = load_list("offs_list", offs)
-        load_live_rows(nc.sync, w2_plane, w2_scales[0])
-        w1_raw_words = keep.tile([P, 2 * H], U8, name="w1_raw_words", align_bytes=64)
-        nc.sync.dma_start(out=w1_raw_words[:].bitcast(I32), in_=w1_words[0].bitcast(I32))
-        load_live_rows(nc.sync, w1_plane, w1_scales[0])
+        w2_plane = sbuf("w2_plane", [P, H], U8)
+        load_plane(w2_plane, w2_scales[0])
         k1_list = load_list("k1_list", k1)
         d_rows = d_scales[0].rearrange("(r e) c -> e r c", e=2)
         for e in range(2):
             nc.sync.dma_start(out=d_byte_table[e:P:16, :].bitcast(I32), in_=d_rows[e].bitcast(I32))
+        w1_codes = load("w1_codes", [P, 2 * H], U8, w1_words[0].bitcast(I32))
         n2_list = load_list("n2_list", n2)
         n3_list = load_list("n3_list", n3)
+        w1_plane = sbuf("w1_plane", [P, H], U8)
+        load_plane(w1_plane, w1_scales[0])
         n1_list = load_list("n1_list", n1)
-        gain = keep.tile([P, PACK], F32, name="gain")
-        nc.sync.dma_start(out=gain[:], in_=gs.rearrange("(p t) o -> p (t o)", t=PACK))
-        d_word_table = keep.tile([P, G], U32, name="d_word_table", align_bytes=64)
-        nc.sync.dma_start(out=d_word_table[:].bitcast(I32), in_=d_words[0].rearrange("p c r -> p (c r)").bitcast(I32))
+        gain = sbuf("gain", [P, SLOTS], F32)
+        nc.sync.dma_start(out=gain[:], in_=gs.rearrange("(p t) o -> p (t o)", t=SLOTS))
+        d_word_table = load("d_word_table", [P, G], U32, word_rows(d_words[0]))
         n4_list = load_list("n4_list", n4)
         n5_list = load_list("n5_list", n5)
 
-        def pick(name, table, offsets, dtype):
-            tile = keep.tile([P, S], dtype, name=name, align_bytes=64)
-            nc.vector.tensor_copy(tile[:], table[:].indirect(offsets[:]))
-            return tile
-
-        def deal(name, source, per_column, dtype):
-            tile = keep.tile([P, H * per_column], dtype, name=name, align_bytes=64)
-            nc.vector.tensor_copy(
-                tile[:].rearrange("p (t m b) -> p t m b", t=PACK, b=per_column),
-                source[:].rearrange("p (m t b) -> p t m b", t=PACK, b=per_column),
-            )
-            return tile
-
-        def turned_product(name, words, plane, token_list):
-            token_bytes = pick(name + "_token_bytes", x_byte_table, token_list, U8)
-            token_words = pick(name + "_token_words", x_word_table, token_list, U32)
+        def turned_product(name, codes, plane, token_list, pieces, banks):
+            token_bytes = sbuf(name + "_token_bytes", [P, S], U8)
+            nc.vector.tensor_copy(token_bytes[:], x_byte_table[:].indirect(token_list[:]))
+            token_words = sbuf(name + "_token_words", [P, S], U32)
+            for lo, hi in pieces:
+                nc.vector.tensor_copy(token_words[:, lo:hi], x_word_table[:].indirect(places(token_list, lo, hi)))
             turned = []
-            for u in range(S // P):
-                bank = psum.tile([P, H], F32, name="bank")
+            for u, number in enumerate(banks):
+                product = bank(number, H)
                 nc.tensor.matmul_mx(
-                    out=bank[:],
+                    out=product[:],
                     lhsT=token_words[:, P * u : P * (u + 1)].bitcast(FP8X4),
                     lhsT_scale=token_bytes[:, P * u : P * (u + 1)],
-                    rhs=words[:].bitcast(FP4X4),
+                    rhs=codes[:].bitcast(FP4X4),
                     rhs_scale=plane[:],
                     start=True,
                     stop=True,
                 )
-                dealt = keep.tile([P, PACK, P], F32, name="%s_turned%d" % (name, u))
-                nc.scalar.copy(dealt[:], bank[:].rearrange("p (m t) -> p t m", t=PACK))
-                turned.append(dealt)
+                by_slot = sbuf("%s_turned%d" % (name, u), [P, SLOTS, P], F32)
+                nc.scalar.copy(by_slot[:], product[:].rearrange("p (m t) -> p t m", t=SLOTS))
+                turned.append(by_slot)
             return turned
 
-        def turn_back(turned, t):
-            bank = psum.tile([P, S], F32, name="bank")
-            for u in range(S // P):
-                nc.tensor.transpose(bank[:, P * u : P * (u + 1)], turned[u][:, t, :], identity[:])
-            return bank
+        def turn_back(turned, t, number):
+            rows = bank(number, S)
+            for u, by_slot in enumerate(turned):
+                nc.tensor.transpose(rows[:, P * u : P * (u + 1)], by_slot[:, t, :], identity[:])
+            return rows
 
-        d_win, y_win, y_plain = [], [], []
+        d_window, y_window, y_plain = {}, {}, {}
 
-        def d_rows_out(t):
-            bank = turn_back(d_turned, t)
-            win = keep.tile([P, WIDE], F32, name="d_win%d" % t)
-            nc.scalar.copy(win[:, :S], bank[:])
-            d_win.append(win)
+        def d_slot(t):
+            rows = turn_back(d_turned, t, SLOTS + t)
+            d_window[t] = sbuf("d_window%d" % t, [P, WIDE], F32)
+            nc.scalar.copy(d_window[t][:, :S], rows[:])
 
-        def y_rows_out(t):
-            bank = turn_back(y_turned, t)
-            win = keep.tile([P, WIDE], F32, name="y_win%d" % t)
-            plain = keep.tile([P, S], F32, name="y_plain%d" % t)
-            nc.scalar.activation(win[:, :S], bank[:], COPY, scale=-0.5)
-            nc.scalar.copy(plain[:], bank[:])
-            y_win.append(win)
-            y_plain.append(plain)
+        def y_slot(t):
+            rows = turn_back(y_turned, t, t % LAST)
+            y_window[t] = sbuf("y_window%d" % t, [P, WIDE], F32)
+            y_plain[t] = sbuf("y_plain%d" % t, [P, S], F32)
+            nc.scalar.activation(y_window[t][:, :S], rows[:], COPY, scale=-0.5)
+            nc.scalar.copy(y_plain[t][:], rows[:])
 
-        d_turned = turned_product("w2", w2_raw_words, w2_plane, two_list)
-        d_rows_out(0)
-        d_rows_out(1)
-        y_turned = turned_product("w1", w1_raw_words, w1_plane, offs_list)
-        y_rows_out(0)
-        d_rows_out(2)
-        y_rows_out(1)
-        d_rows_out(3)
-        y_rows_out(2)
-        y_rows_out(3)
+        d_turned = turned_product("d", w2_codes, w2_plane, two_list, HALVES, (0, 1, 2, 3))
+        d_slot(0)
+        d_slot(1)
+        y_turned = turned_product("y", w1_codes, w1_plane, offs_list, WHOLE, (3, 4, 5, 3))
+        for t in range(SLOTS):
+            y_slot(t)
+            if t + 2 < SLOTS:
+                d_slot(t + 2)
 
-        code_bytes = pick("code_bytes", d_byte_table, k1_list, U8)
-        code_dealt_bytes = deal("code_dealt_bytes", code_bytes, 1, U8)
-        for row, part in enumerate((0, 1, 16, 17)):
-            nc.sync.dma_start(out=code_plane[row:P:32, :].bitcast(I32), in_=code_dealt_bytes[part:P:32, :].bitcast(I32))
+        code_bytes = sbuf("code_bytes", [P, H], U8)
+        nc.vector.tensor_copy(code_bytes[:], d_byte_table[:].indirect(k1_list[:]))
+        code_bytes_by_slot = sbuf("code_bytes_by_slot", [P, SLOTS, P], U8)
+        nc.vector.tensor_copy(code_bytes_by_slot[:], code_bytes[:].rearrange("p (m t) -> p t m", t=SLOTS))
+        sorted_bytes = code_bytes_by_slot[:].rearrange("p t m -> p (t m)").bitcast(I32)
+        for row, partition in enumerate((0, 1, 16, 17)):
+            nc.sync.dma_start(out=code_plane[row:P:32, :].bitcast(I32), in_=sorted_bytes[partition:P:32, :])
 
-        z_bf = keep.tile([P, S, PACK], BF16, name="z_bf", align_bytes=64)
-        units = [(t, 0, S) for t in range(PACK - 1)] + [(PACK - 1, lo, hi) for lo, hi in Z_CHUNKS]
-        got = {}
+        z_rounded = {lo: sbuf("z_rounded%d" % lo, [P, hi - lo, SLOTS], BF16) for lo, hi in CHUNKS}
+        at_n2, at_n3, lessened, low = {}, {}, {}, {}
+        after_third_minimum, after_last_minimum = "after_third_minimum", "after_last_minimum"
 
-        def look_up_d(i):
-            t, lo, hi = units[i]
-            last = i == len(units) - 1
-            at_n2 = keep.tile([P, hi - lo], F32, name="at_n2_%d" % i, tag="held" if last else "at_n2_%d" % i, align_bytes=64)
-            at_n3 = keep.tile([P, hi - lo], F32, name="at_n3_%d" % i)
-            nc.vector.tensor_copy(at_n2[:], d_win[t][:].indirect(n2_list[:, lo // 16 : hi // 16]))
-            nc.vector.tensor_copy(at_n3[:], d_win[t][:].indirect(n3_list[:, lo // 16 : hi // 16]))
-            got["n2", i] = at_n2
-            got["n3", i] = at_n3
+        def look_up_n2(t):
+            at_n2[t] = sbuf("at_n2_%d" % t, [P, S], F32, after_last_minimum if t == LAST else None)
+            nc.vector.tensor_copy(at_n2[t][:], d_window[t][:].indirect(n2_list[:]))
 
-        def look_up_y(i):
-            t, lo, hi = units[i]
-            lessened = keep.tile([P, hi - lo], F32, name="lessened%d" % i)
-            nc.vector.tensor_tensor(
-                lessened[:], y_win[t][:].indirect(n1_list[:, lo // 16 : hi // 16]), y_plain[t][:, lo:hi], ALU.add
-            )
-            got["n1", i] = lessened
+        def look_up_n3(t):
+            hi = HALF if t == LAST else S
+            at_n3[t] = sbuf("at_n3_%d" % t, [P, hi], F32, after_third_minimum if t == LAST else None)
+            nc.vector.tensor_copy(at_n3[t][:], d_window[t][:].indirect(places(n3_list, 0, hi)))
 
-        def smaller(i):
-            t, lo, hi = units[i]
-            low = keep.tile([P, hi - lo], F32, name="low%d" % i)
-            nc.vector.tensor_tensor(low[:], got["n1", i][:], got["n2", i][:], ALU.min)
-            got["low", i] = low
+        def look_up_n1(t):
+            lessened[t] = sbuf("lessened%d" % t, [P, S], F32, after_third_minimum if t == LAST - 1 else None)
+            nc.vector.tensor_tensor(lessened[t][:], y_window[t][:].indirect(n1_list[:]), y_plain[t][:], ALU.add)
 
-        def larger(i):
-            t, lo, hi = units[i]
-            clamped = keep.tile([P, hi - lo], F32, name="clamped%d" % i)
-            nc.vector.tensor_tensor(clamped[:], got["low", i][:], got["n3", i][:], ALU.max)
-            nc.scalar.activation(z_bf[:, lo:hi, t], clamped[:], COPY, scale=gain[:, t : t + 1])
+        def minimum(t):
+            low[t] = sbuf("low%d" % t, [P, S], F32)
+            for lo, hi in HALVES if t == LAST else WHOLE:
+                nc.vector.tensor_tensor(low[t][:, lo:hi], lessened[t][:, lo:hi], at_n2[t][:, lo:hi], ALU.min)
 
-        z_words = keep.tile([P, S], U32, name="z_words", align_bytes=64)
-        z_plane = keep.tile([P, S], U8, name="z_plane", align_bytes=64)
+        def maximum(t, clamped, floor, lo, hi):
+            nc.vector.tensor_tensor(clamped[:, lo:hi], low[t][:, lo:hi], floor[:, lo:hi], ALU.max)
+            for a, b in CHUNKS:
+                if lo <= a and b <= hi:
+                    nc.scalar.activation(z_rounded[a][:, :, t], clamped[:, a:b], COPY, scale=gain[:, t : t + 1])
 
-        def quantise_z(lo, hi):
-            nc.vector.quantize_mx(
-                out=z_words[:, lo:hi].bitcast(FP8X4),
-                scales=z_plane[:, lo:hi],
-                in_=z_bf[:, lo:hi, :].rearrange("p j t -> p (j t)"),
-            )
-
-        look_up_d(0)
-        for i in range(len(units)):
-            if i + 1 < len(units):
-                look_up_d(i + 1)
-            look_up_y(i)
-            if i > 0:
-                larger(i - 1)
-            smaller(i)
-        larger(len(units) - 1)
-        code_words = keep.tile([P, S], U32, name="code_words", tag="held", align_bytes=64)
-        nc.vector.tensor_copy(code_words[:], d_word_table[:].indirect(k1_list[:]))
-        quantise_z(*Z_CHUNKS[0])
-        code_dealt = deal("code_dealt", code_words, 1, U32)
-        quantise_z(*Z_CHUNKS[1])
-
-        h_win, h_half = [], []
-        for t in range(PACK):
-            bank = psum.tile([P, S], F32, name="bank")
-            win = keep.tile([P, WIDE], F32, name="h_win%d" % t)
-            half = keep.tile([P, S], F32, name="h_half%d" % t)
-            for lo, hi in Z_CHUNKS:
-                nc.tensor.matmul_mx(
-                    out=bank[:, lo:hi],
-                    lhsT=code_dealt[:, P * t : P * (t + 1)].bitcast(FP8X4),
-                    lhsT_scale=code_plane[:, P * t : P * (t + 1)],
-                    rhs=z_words[:, lo:hi].bitcast(FP8X4),
-                    rhs_scale=z_plane[:, lo:hi],
-                    start=True,
-                    stop=True,
-                )
-            nc.scalar.activation(win[:, :S], bank[:], COPY, scale=0.0625)
-            h_win.append(win)
-            h_half.append((half, bank))
-        for half, bank in h_half:
-            nc.scalar.activation(half[:], bank[:], COPY, scale=0.03125)
-
-        st_win = []
-        at_n4 = []
-        for t in range(PACK + 1):
-            if t < PACK:
-                got = work.tile([P, S], F32, name="at_n4")
-                nc.vector.tensor_copy(got[:], h_win[t][:].indirect(n4_list[:]))
-                at_n4.append(got)
+        d_look_ups = [(look_up, t) for t in range(SLOTS) for look_up in (look_up_n2, look_up_n3)]
+        for look_up, t in d_look_ups[:SLOTS]:
+            look_up(t)
+        for t in range(SLOTS):
+            look_up_n1(t)
             if t > 0:
-                win = keep.tile([P, S], F32, name="st_win%d" % (t - 1))
-                nc.vector.tensor_tensor(win[:], at_n4[t - 1][:], h_win[t - 1][:, :S], ALU.max)
-                st_win.append(win)
+                maximum(t - 1, sbuf("clamped%d" % (t - 1), [P, S], F32), at_n3[t - 1], 0, S)
+            look_up, ahead = d_look_ups[SLOTS + t]
+            look_up(ahead)
+            minimum(t)
+        clamped = sbuf("clamped%d" % LAST, [P, S], F32)
+        maximum(LAST, clamped, at_n3[LAST], 0, HALF)
+        at_n3_rest = sbuf("at_n3_rest", [P, S], F32, after_last_minimum)
+        nc.vector.tensor_copy(at_n3_rest[:, HALF:], d_window[LAST][:].indirect(places(n3_list, HALF, S)))
+        for lo, hi in CHUNKS[1:]:
+            maximum(LAST, clamped, at_n3_rest, lo, hi)
 
-        out_rows = out_0.rearrange("(p t) j -> p t j", t=PACK)
-        out_words = out_1[0].rearrange("p c r -> p (c r)").bitcast(I32)
-        o_plane = keep.tile([P, S], U8, name="o_plane", align_bytes=64)
-        pending = None
-        for c, (lo, hi) in enumerate(OUT_CHUNKS):
-            n = hi - lo
-            result = keep.tile([P, PACK, n], F32, name="result%d" % c)
-            rounded = keep.tile([P, n, PACK], BF16, name="rounded%d" % c, align_bytes=64)
-            o_words = keep.tile([P, n], U32, name="o_words%d" % c, align_bytes=64)
-            for t in range(PACK):
+        code_words = sbuf("code_words", [P, H], U32, after_third_minimum)
+        nc.vector.tensor_copy(code_words[:], d_word_table[:].indirect(k1_list[:]))
+        words_by_slot = code_words[:].rearrange("p (m t) -> p t m", t=SLOTS)
+        z_words = sbuf("z_words", [P, S], U32)
+        z_plane = sbuf("z_plane", [P, S], U8)
+        code_pairs = [sbuf("code_pair0", [P, 2, P], U32)]
+        for lo, hi in CHUNKS:
+            quantise(z_words[:, lo:hi], z_plane[:, lo:hi], z_rounded[lo])
+            if lo == 0:
+                nc.vector.tensor_copy(code_pairs[0][:], words_by_slot[:, :2, :])
+        code_pairs.append(sbuf("code_pair1", [P, 2, P], U32, "z_rounded%d" % CHUNKS[-1][0]))
+        nc.vector.tensor_copy(code_pairs[1][:], words_by_slot[:, 2:, :])
+
+        h_window = {t: sbuf("h_window%d" % t, [P, WIDE], F32) for t in range(SLOTS)}
+        h_passes = [(t, lo, hi) for t in range(SLOTS) for lo, hi in (CHUNKS if t == 0 else WHOLE)]
+        for number, (t, lo, hi) in enumerate(h_passes):
+            product = bank(number, hi - lo)
+            nc.tensor.matmul_mx(
+                out=product[:],
+                lhsT=code_pairs[t // 2][:, t % 2, :].bitcast(FP8X4),
+                lhsT_scale=code_plane[:, P * t : P * (t + 1)],
+                rhs=z_words[:, lo:hi].bitcast(FP8X4),
+                rhs_scale=z_plane[:, lo:hi],
+                start=True,
+                stop=True,
+            )
+            nc.scalar.activation(h_window[t][:, lo:hi], product[:], COPY, scale=0.0625)
+
+        at_n4, st_window, h_half = {}, {}, {}
+        for step in range(SLOTS + 1):
+            if step < SLOTS:
+                at_n4[step] = sbuf("at_n4_%d" % step, [P, S], F32)
+                nc.vector.tensor_copy(at_n4[step][:], h_window[step][:].indirect(n4_list[:]))
+            if step > 0:
+                t = step - 1
+                st_window[t] = sbuf("st_window%d" % t, [P, S], F32)
+                nc.vector.tensor_tensor(st_window[t][:], at_n4[t][:], h_window[t][:, :S], ALU.max)
+                h_half[t] = sbuf("h_half%d" % t, [P, S], F32, "at_n4_%d" % t)
+                nc.scalar.activation(h_half[t][:], h_window[t][:, :S], COPY, scale=0.5)
+
+        out_rows = out_0.rearrange("(p t) j -> p t j", t=SLOTS)
+        out_words = word_rows(out_1[0])
+        out_plane = sbuf("out_plane", [P, S], U8)
+        out_rounded = {lo: sbuf("out_rounded%d" % lo, [P, hi - lo, SLOTS], BF16) for lo, hi in CHUNKS}
+
+        def hand_on(lo, hi):
+            words = sbuf("out_codes%d" % lo, [P, hi - lo], U32)
+            quantise(words[:], out_plane[:, lo:hi], out_rounded[lo])
+            nc.sync.dma_start(out=out_words[:, lo:hi], in_=words[:].bitcast(I32))
+
+        for c, (lo, hi) in enumerate(CHUNKS):
+            result = sbuf("result%d" % lo, [P, SLOTS, hi - lo], F32)
+            for t in range(SLOTS):
                 nc.vector.tensor_tensor(
-                    result[:, t, :], st_win[t][:].indirect(n5_list[:, lo // 16 : hi // 16]), h_half[t][0][:, lo:hi], ALU.subtract
+                    result[:, t, :], st_window[t][:].indirect(places(n5_list, lo, hi)), h_half[t][:, lo:hi], ALU.subtract
                 )
-                nc.scalar.copy(rounded[:, :, t], result[:, t, :])
-                if t == 2 and pending is not None:
-                    pending()
+                if hi == S and t % 2:
+                    nc.scalar.copy(
+                        out_rounded[lo][:, :, t - 1 : t + 1], result[:, t - 1 : t + 1, :].rearrange("p t j -> p j t")
+                    )
+            if hi < S:
+                nc.scalar.copy(
+                    out_rounded[lo][:].rearrange("p (c i) t -> p c t i", i=4),
+                    result[:].rearrange("p t (c i) -> p c t i", i=4),
+                )
+            if c > 0:
+                hand_on(*CHUNKS[c - 1])
             nc.sync.dma_start(out=out_rows[:, :, lo:hi], in_=result[:])
-
-            def quantise(lo=lo, hi=hi, rounded=rounded, o_words=o_words):
-                nc.vector.quantize_mx(
-                    out=o_words[:].bitcast(FP8X4), scales=o_plane[:, lo:hi], in_=rounded[:].rearrange("p j t -> p (j t)")
-                )
-                nc.sync.dma_start(out=out_words[:, lo:hi], in_=o_words[:].bitcast(I32))
-
-            pending = quantise
-        pending()
-        for q in range(4):
-            queue = nc.scalar if q % 2 else nc.sync
-            queue.dma_start(out=out_2[0][4 * q : 4 * q + 4, :].bitcast(I32), in_=o_plane[32 * q : 32 * q + 4, :].bitcast(I32))
+        hand_on(*CHUNKS[-1])
+        for q, (partitions, target) in enumerate(plane_rows(out_plane, out_2[0])):
+            (nc.scalar if q % 2 else nc.sync).dma_start(out=target, in_=partitions)

@@ -48,13 +48,13 @@ def tile_picked_twqclampbhopb_none_po_kernel(
     with ExitStack() as ctx:
         lists = ctx.enter_context(tc.tile_pool(name="lists", bufs=1))
         keep = ctx.enter_context(tc.tile_pool(name="keep", bufs=1))
-        psum = ctx.enter_context(tc.psum_pool(name="psum", bufs=1))
+        psum = ctx.enter_context(tc.psum_pool(name="psum", bufs=8))
 
         def sbuf(name, shape, dtype, tag=None):
             return keep.tile(shape, dtype, name=name, tag=tag or name, align_bytes=64)
 
-        def bank(number, width):
-            return psum.tile([P, width], F32, name="bank%d" % number)
+        def bank(width):
+            return psum.tile([P, width], F32, name="bank")
 
         def zeroed_bytes(name, width, engine):
             tile = sbuf(name, [P, width], U8)
@@ -82,7 +82,6 @@ def tile_picked_twqclampbhopb_none_po_kernel(
         identity = sbuf("identity", [P, P], F32)
         make_identity(nc, identity[:])
         d_byte_table = zeroed_bytes("d_byte_table", G, nc.vector)
-        code_plane = zeroed_bytes("code_plane", H, nc.vector)
 
         w2_codes = load("w2_codes", [P, 2 * H], U8, w2_words[0].bitcast(I32))
         two_list = load_list("two_list", two)
@@ -107,15 +106,15 @@ def tile_picked_twqclampbhopb_none_po_kernel(
         n4_list = load_list("n4_list", n4)
         n5_list = load_list("n5_list", n5)
 
-        def turned_product(name, codes, plane, token_list, pieces, banks):
+        def turned_product(name, codes, plane, token_list, pieces):
             token_bytes = sbuf(name + "_token_bytes", [P, S], U8)
             nc.vector.tensor_copy(token_bytes[:], x_byte_table[:].indirect(token_list[:]))
             token_words = sbuf(name + "_token_words", [P, S], U32)
             for lo, hi in pieces:
                 nc.vector.tensor_copy(token_words[:, lo:hi], x_word_table[:].indirect(places(token_list, lo, hi)))
             turned = []
-            for u, number in enumerate(banks):
-                product = bank(number, H)
+            for u in range(S // P):
+                product = bank(H)
                 nc.tensor.matmul_mx(
                     out=product[:],
                     lhsT=token_words[:, P * u : P * (u + 1)].bitcast(FP8X4),
@@ -130,8 +129,8 @@ def tile_picked_twqclampbhopb_none_po_kernel(
                 turned.append(by_slot)
             return turned
 
-        def turn_back(turned, t, number):
-            rows = bank(number, S)
+        def turn_back(turned, t):
+            rows = bank(S)
             for u, by_slot in enumerate(turned):
                 nc.tensor.transpose(rows[:, P * u : P * (u + 1)], by_slot[:, t, :], identity[:])
             return rows
@@ -139,21 +138,21 @@ def tile_picked_twqclampbhopb_none_po_kernel(
         d_window, y_window, y_plain = {}, {}, {}
 
         def d_slot(t):
-            rows = turn_back(d_turned, t, SLOTS + t)
+            rows = turn_back(d_turned, t)
             d_window[t] = sbuf("d_window%d" % t, [P, WIDE], F32)
             nc.scalar.copy(d_window[t][:, :S], rows[:])
 
         def y_slot(t):
-            rows = turn_back(y_turned, t, t % LAST)
+            rows = turn_back(y_turned, t)
             y_window[t] = sbuf("y_window%d" % t, [P, WIDE], F32)
             y_plain[t] = sbuf("y_plain%d" % t, [P, S], F32)
             nc.scalar.activation(y_window[t][:, :S], rows[:], COPY, scale=-0.5)
             nc.scalar.copy(y_plain[t][:], rows[:])
 
-        d_turned = turned_product("d", w2_codes, w2_plane, two_list, HALVES, (0, 1, 2, 3))
+        d_turned = turned_product("d", w2_codes, w2_plane, two_list, HALVES)
         d_slot(0)
         d_slot(1)
-        y_turned = turned_product("y", w1_codes, w1_plane, offs_list, WHOLE, (3, 4, 5, 3))
+        y_turned = turned_product("y", w1_codes, w1_plane, offs_list, WHOLE)
         for t in range(SLOTS):
             y_slot(t)
             if t + 2 < SLOTS:
@@ -164,6 +163,7 @@ def tile_picked_twqclampbhopb_none_po_kernel(
         code_bytes_by_slot = sbuf("code_bytes_by_slot", [P, SLOTS, P], U8)
         nc.vector.tensor_copy(code_bytes_by_slot[:], code_bytes[:].rearrange("p (m t) -> p t m", t=SLOTS))
         sorted_bytes = code_bytes_by_slot[:].rearrange("p t m -> p (t m)").bitcast(I32)
+        code_plane = sbuf("code_plane", [P, H], U8)
         for row, partition in enumerate((0, 1, 16, 17)):
             nc.sync.dma_start(out=code_plane[row:P:32, :].bitcast(I32), in_=sorted_bytes[partition:P:32, :])
 
@@ -227,8 +227,8 @@ def tile_picked_twqclampbhopb_none_po_kernel(
 
         h_window = {t: sbuf("h_window%d" % t, [P, WIDE], F32) for t in range(SLOTS)}
         h_passes = [(t, lo, hi) for t in range(SLOTS) for lo, hi in (CHUNKS if t == 0 else WHOLE)]
-        for number, (t, lo, hi) in enumerate(h_passes):
-            product = bank(number, hi - lo)
+        for t, lo, hi in h_passes:
+            product = bank(hi - lo)
             nc.tensor.matmul_mx(
                 out=product[:],
                 lhsT=code_pairs[t // 2][:, t % 2, :].bitcast(FP8X4),

from contextlib import ExitStack

import concourse.mybir as mybir
from concourse.masks import make_identity

F32 = mybir.dt.float32
BF16 = mybir.dt.bfloat16
I32 = mybir.dt.int32
U32 = mybir.dt.uint32
U16 = mybir.dt.uint16
U8 = mybir.dt.uint8
FP8X4 = mybir.dt.float8_e4m3fn_x4
FP4X4 = mybir.dt.float4_e2m1fn_x4
ALU = mybir.AluOpType
COPY = mybir.ActivationFunctionType.Copy

P = 128
SLOTS = 4
LAST = SLOTS - 1
PER_COLUMN = 16
K, T, S, H, G = 512, 1024, 512, 512, 2048
FLOPS = 3 * 2 * K * H * S

WIDE = 2 * S
HALF = S // 2
WHOLE = ((0, S),)
HALVES = ((0, HALF), (HALF, S))
CHUNKS = ((0, HALF), (HALF, HALF + P), (HALF + P, S))


def plane_rows(plane, rows):
    return [(plane[32 * q : 32 * q + 4, :].bitcast(I32), rows[4 * q : 4 * q + 4, :].bitcast(I32)) for q in range(4)]


def word_rows(words):
    return words.rearrange("p c r -> p (c r)").bitcast(I32)


def places(offsets, lo, hi):
    return offsets[:, lo // PER_COLUMN : hi // PER_COLUMN]


def tile_picked_twqclampbhopb_none_po_kernel(
    tc, x_words, x_scales, w1_words, w1_scales, w2_words, w2_scales, gs, d_words, d_scales,
    offs, two, n1, n2, n3, k1, n4, n5, out_0, out_1, out_2,
):
    nc = tc.nc
    with ExitStack() as ctx:
        lists = ctx.enter_context(tc.tile_pool(name="lists", bufs=1))
        keep = ctx.enter_context(tc.tile_pool(name="keep", bufs=1))
        psum = ctx.enter_context(tc.psum_pool(name="psum", bufs=8))

        def sbuf(name, shape, dtype, tag=None):
            return keep.tile(shape, dtype, name=name, tag=tag or name, align_bytes=64)

        def bank(width):
            return psum.tile([P, width], F32, name="bank")

        def zeroed_bytes(name, width, engine):
            tile = sbuf(name, [P, width], U8)
            engine.memset(tile[:].bitcast(I32), 0)
            return tile

        def load(name, shape, dtype, source):
            tile = sbuf(name, shape, dtype)
            nc.sync.dma_start(out=tile[:].bitcast(I32), in_=source)
            return tile

        def load_list(name, source):
            tile = lists.tile([P, S // PER_COLUMN], U16, name=name)
            nc.sync.dma_start(tile[:], source)
            return tile

        def load_plane(plane, rows):
            for partitions, source in plane_rows(plane, rows):
                nc.sync.dma_start(out=partitions, in_=source)

        def quantise(words, plane, rounded):
            nc.vector.quantize_mx(out=words.bitcast(FP8X4), scales=plane, in_=rounded[:].rearrange("p j t -> p (j t)"))

        x_byte_table = zeroed_bytes("x_byte_table", T, nc.gpsimd)
        identity = sbuf("identity", [P, P], F32)
        make_identity(nc, identity[:])
        d_byte_table = zeroed_bytes("d_byte_table", G, nc.vector)

        w2_codes = load("w2_codes", [P, 2 * H], U8, w2_words[0].bitcast(I32))
        two_list = load_list("two_list", two)
        load_plane(x_byte_table, x_scales[0])
        x_word_table = load("x_word_table", [P, T], U32, word_rows(x_words[0]))
        offs_list = load_list("offs_list", offs)
        w2_plane = sbuf("w2_plane", [P, H], U8)
        load_plane(w2_plane, w2_scales[0])
        k1_list = load_list("k1_list", k1)
        d_rows = d_scales[0].rearrange("(r e) c -> e r c", e=2)
        for e in range(2):
            nc.sync.dma_start(out=d_byte_table[e:P:16, :].bitcast(I32), in_=d_rows[e].bitcast(I32))
        w1_codes = load("w1_codes", [P, 2 * H], U8, w1_words[0].bitcast(I32))
        n2_list = load_list("n2_list", n2)
        n3_list = load_list("n3_list", n3)
        w1_plane = sbuf("w1_plane", [P, H], U8)
        load_plane(w1_plane, w1_scales[0])
        n1_list = load_list("n1_list", n1)
        gain = sbuf("gain", [P, SLOTS], F32)
        nc.sync.dma_start(out=gain[:], in_=gs.rearrange("(p t) o -> p (t o)", t=SLOTS))
        d_word_table = load("d_word_table", [P, G], U32, word_rows(d_words[0]))
        n4_list = load_list("n4_list", n4)
        n5_list = load_list("n5_list", n5)

        def turned_product(name, codes, plane, token_list, pieces):
            token_bytes = sbuf(name + "_token_bytes", [P, S], U8)
            nc.vector.tensor_copy(token_bytes[:], x_byte_table[:].indirect(token_list[:]))
            token_words = sbuf(name + "_token_words", [P, S], U32)
            for lo, hi in pieces:
                nc.vector.tensor_copy(token_words[:, lo:hi], x_word_table[:].indirect(places(token_list, lo, hi)))
            turned = []
            for u in range(S // P):
                product = bank(H)
                nc.tensor.matmul_mx(
                    out=product[:],
                    lhsT=token_words[:, P * u : P * (u + 1)].bitcast(FP8X4),
                    lhsT_scale=token_bytes[:, P * u : P * (u + 1)],
                    rhs=codes[:].bitcast(FP4X4),
                    rhs_scale=plane[:],
                    start=True,
                    stop=True,
                )
                by_slot = sbuf("%s_turned%d" % (name, u), [P, SLOTS, P], F32)
                nc.scalar.copy(by_slot[:], product[:].rearrange("p (m t) -> p t m", t=SLOTS))
                turned.append(by_slot)
            return turned

        def turn_back(turned, t):
            rows = bank(S)
            for u, by_slot in enumerate(turned):
                nc.tensor.transpose(rows[:, P * u : P * (u + 1)], by_slot[:, t, :], identity[:])
            return rows

        d_window, y_window, y_plain = {}, {}, {}

        def d_slot(t):
            rows = turn_back(d_turned, t)
            d_window[t] = sbuf("d_window%d" % t, [P, WIDE], F32)
            nc.scalar.copy(d_window[t][:, :S], rows[:])

        def y_slot(t):
            rows = turn_back(y_turned, t)
            y_window[t] = sbuf("y_window%d" % t, [P, WIDE], F32)
            y_plain[t] = sbuf("y_plain%d" % t, [P, S], F32)
            nc.scalar.activation(y_window[t][:, :S], rows[:], COPY, scale=-0.5)
            nc.scalar.copy(y_plain[t][:], rows[:])

        d_turned = turned_product("d", w2_codes, w2_plane, two_list, HALVES)
        d_slot(0)
        d_slot(1)
        y_turned = turned_product("y", w1_codes, w1_plane, offs_list, WHOLE)
        for t in range(SLOTS):
            y_slot(t)
            if t + 2 < SLOTS:
                d_slot(t + 2)

        code_bytes = sbuf("code_bytes", [P, H], U8)
        nc.vector.tensor_copy(code_bytes[:], d_byte_table[:].indirect(k1_list[:]))
        code_bytes_by_slot = sbuf("code_bytes_by_slot", [P, SLOTS, P], U8)
        nc.vector.tensor_copy(code_bytes_by_slot[:], code_bytes[:].rearrange("p (m t) -> p t m", t=SLOTS))
        sorted_bytes = code_bytes_by_slot[:].rearrange("p t m -> p (t m)").bitcast(I32)
        code_plane = sbuf("code_plane", [P, H], U8)
        for row, partition in enumerate((0, 1, 16, 17)):
            nc.sync.dma_start(out=code_plane[row:P:32, :].bitcast(I32), in_=sorted_bytes[partition:P:32, :])

        z_rounded = {lo: sbuf("z_rounded%d" % lo, [P, hi - lo, SLOTS], BF16) for lo, hi in CHUNKS}
        at_n2, at_n3, lessened, low = {}, {}, {}, {}
        after_third_minimum, after_last_minimum = "after_third_minimum", "after_last_minimum"

        def look_up_n2(t):
            at_n2[t] = sbuf("at_n2_%d" % t, [P, S], F32, after_last_minimum if t == LAST else None)
            nc.vector.tensor_copy(at_n2[t][:], d_window[t][:].indirect(n2_list[:]))

        def look_up_n3(t):
            hi = HALF if t == LAST else S
            at_n3[t] = sbuf("at_n3_%d" % t, [P, hi], F32, after_third_minimum if t == LAST else None)
            nc.vector.tensor_copy(at_n3[t][:], d_window[t][:].indirect(places(n3_list, 0, hi)))

        def look_up_n1(t):
            lessened[t] = sbuf("lessened%d" % t, [P, S], F32, after_third_minimum if t == LAST - 1 else None)
            nc.vector.tensor_tensor(lessened[t][:], y_window[t][:].indirect(n1_list[:]), y_plain[t][:], ALU.add)

        def minimum(t):
            low[t] = sbuf("low%d" % t, [P, S], F32)
            for lo, hi in HALVES if t == LAST else WHOLE:
                nc.vector.tensor_tensor(low[t][:, lo:hi], lessened[t][:, lo:hi], at_n2[t][:, lo:hi], ALU.min)

        def maximum(t, clamped, floor, lo, hi):
            nc.vector.tensor_tensor(clamped[:, lo:hi], low[t][:, lo:hi], floor[:, lo:hi], ALU.max)
            for a, b in CHUNKS:
                if lo <= a and b <= hi:
                    nc.scalar.activation(z_rounded[a][:, :, t], clamped[:, a:b], COPY, scale=gain[:, t : t + 1])

        d_look_ups = [(look_up, t) for t in range(SLOTS) for look_up in (look_up_n2, look_up_n3)]
        for look_up, t in d_look_ups[:SLOTS]:
            look_up(t)
        for t in range(SLOTS):
            look_up_n1(t)
            if t > 0:
                maximum(t - 1, sbuf("clamped%d" % (t - 1), [P, S], F32), at_n3[t - 1], 0, S)
            look_up, ahead = d_look_ups[SLOTS + t]
            look_up(ahead)
            minimum(t)
        clamped = sbuf("clamped%d" % LAST, [P, S], F32)
        maximum(LAST, clamped, at_n3[LAST], 0, HALF)
        at_n3_rest = sbuf("at_n3_rest", [P, S], F32, after_last_minimum)
        nc.vector.tensor_copy(at_n3_rest[:, HALF:], d_window[LAST][:].indirect(places(n3_list, HALF, S)))
        for lo, hi in CHUNKS[1:]:
            maximum(LAST, clamped, at_n3_rest, lo, hi)

        code_words = sbuf("code_words", [P, H], U32, after_third_minimum)
        nc.vector.tensor_copy(code_words[:], d_word_table[:].indirect(k1_list[:]))
        words_by_slot = code_words[:].rearrange("p (m t) -> p t m", t=SLOTS)
        z_words = sbuf("z_words", [P, S], U32)
        z_plane = sbuf("z_plane", [P, S], U8)
        code_pairs = [sbuf("code_pair0", [P, 2, P], U32)]
        for lo, hi in CHUNKS:
            quantise(z_words[:, lo:hi], z_plane[:, lo:hi], z_rounded[lo])
            if lo == 0:
                nc.vector.tensor_copy(code_pairs[0][:], words_by_slot[:, :2, :])
        code_pairs.append(sbuf("code_pair1", [P, 2, P], U32, "z_rounded%d" % CHUNKS[-1][0]))
        nc.vector.tensor_copy(code_pairs[1][:], words_by_slot[:, 2:, :])

        h_window = {t: sbuf("h_window%d" % t, [P, WIDE], F32) for t in range(SLOTS)}
        h_passes = [(t, lo, hi) for t in range(SLOTS) for lo, hi in (CHUNKS if t == 0 else WHOLE)]
        for t, lo, hi in h_passes:
            product = bank(hi - lo)
            nc.tensor.matmul_mx(
                out=product[:],
                lhsT=code_pairs[t // 2][:, t % 2, :].bitcast(FP8X4),
                lhsT_scale=code_plane[:, P * t : P * (t + 1)],
                rhs=z_words[:, lo:hi].bitcast(FP8X4),
                rhs_scale=z_plane[:, lo:hi],
                start=True,
                stop=True,
            )
            nc.scalar.activation(h_window[t][:, lo:hi], product[:], COPY, scale=0.0625)

        at_n4, st_window, h_half = {}, {}, {}
        for step in range(SLOTS + 1):
            if step < SLOTS:
                at_n4[step] = sbuf("at_n4_%d" % step, [P, S], F32)
                nc.vector.tensor_copy(at_n4[step][:], h_window[step][:].indirect(n4_list[:]))
            if step > 0:
                t = step - 1
                st_window[t] = sbuf("st_window%d" % t, [P, S], F32)
                nc.vector.tensor_tensor(st_window[t][:], at_n4[t][:], h_window[t][:, :S], ALU.max)
                h_half[t] = sbuf("h_half%d" % t, [P, S], F32, "at_n4_%d" % t)
                nc.scalar.activation(h_half[t][:], h_window[t][:, :S], COPY, scale=0.5)

        out_rows = out_0.rearrange("(p t) j -> p t j", t=SLOTS)
        out_words = word_rows(out_1[0])
        out_plane = sbuf("out_plane", [P, S], U8)
        out_rounded = {lo: sbuf("out_rounded%d" % lo, [P, hi - lo, SLOTS], BF16) for lo, hi in CHUNKS}

        def hand_on(lo, hi):
            words = sbuf("out_codes%d" % lo, [P, hi - lo], U32)
            quantise(words[:], out_plane[:, lo:hi], out_rounded[lo])
            nc.sync.dma_start(out=out_words[:, lo:hi], in_=words[:].bitcast(I32))

        for c, (lo, hi) in enumerate(CHUNKS):
            result = sbuf("result%d" % lo, [P, SLOTS, hi - lo], F32)
            for t in range(SLOTS):
                nc.vector.tensor_tensor(
                    result[:, t, :], st_window[t][:].indirect(places(n5_list, lo, hi)), h_half[t][:, lo:hi], ALU.subtract
                )
                if hi == S and t % 2:
                    nc.scalar.copy(
                        out_rounded[lo][:, :, t - 1 : t + 1], result[:, t - 1 : t + 1, :].rearrange("p t j -> p j t")
                    )
            if hi < S:
                nc.scalar.copy(
                    out_rounded[lo][:].rearrange("p (c i) t -> p c t i", i=4),
                    result[:].rearrange("p t (c i) -> p c t i", i=4),
                )
            if c > 0:
                hand_on(*CHUNKS[c - 1])
            nc.sync.dma_start(out=out_rows[:, :, lo:hi], in_=result[:])
        hand_on(*CHUNKS[-1])
        for q, (partitions, target) in enumerate(plane_rows(out_plane, out_2[0])):
            (nc.scalar if q % 2 else nc.sync).dma_start(out=target, in_=partitions)
